import numpy as np, ml_dtypes
CORES = [9,10,11,14,17,18,19,22,49,50,51,54]
N = 12
TK = 32
def setup_inputs(rng):
    return {"x": rng.standard_normal((N, 128, TK), dtype=np.float32).astype(ml_dtypes.bfloat16), "w1": (rng.standard_normal((N, 128, 128), dtype=np.float32) / 8).astype(ml_dtypes.bfloat16), "w2": (rng.standard_normal((N, 128, 128), dtype=np.float32) / 8).astype(ml_dtypes.bfloat16)}
def setup_inputs_big(rng):
    d = setup_inputs(rng)
    for k in ("x", "w1", "w2"): d[k] = (d[k].astype(np.float32) * 1024.0).astype(d[k].dtype)
    return d
def setup_inputs_small(rng):
    d = setup_inputs(rng)
    for k in ("x", "w1", "w2"): d[k] = (d[k].astype(np.float32) * (1 / 1024.0)).astype(d[k].dtype)
    return d
def setup_inputs_apart(rng):
    d = setup_inputs(rng)
    f = (10.0 ** rng.permutation(np.linspace(-1.5, 1.5, N))).astype(np.float32).reshape(N, 1, 1)
    for k in ("x", "w1", "w2"): d[k] = (d[k].astype(np.float32) * f).astype(d[k].dtype)
    return d
def reference(x, w1, w2):
    X, W1, W2 = x.astype(np.float64), w1.astype(np.float64), w2.astype(np.float64)
    y = np.zeros((N, 128, TK))
    for r in range(N):
        for j in range(N):
            y[r] += W2[j].T @ np.maximum(W1[j].T @ X[r], 0.0)
    return {"y": y.astype(ml_dtypes.bfloat16 if x.dtype != np.float64 else np.float64)}

@@ -1,0 +1,245 @@
+from concourse.bass import DstId, RemoteDMATransfer
+from concourse.mybir import AluOpType
+
+TK = 32
+D = 128
+PER_CHIP = 4
+MAX_A = 3
+MAX_B = 2
+MAX_IN = 3
+
+SCRATCH = {
+    "xa": ("sbuf", [D, TK * (1 + MAX_A)], "bfloat16"),
+    "xb": ("sbuf", [D, TK * MAX_B], "bfloat16"),
+    "W": ("sbuf", [D, 2 * D * PER_CHIP], "bfloat16"),
+    "zeros": ("sbuf", [D, 512], "float32"),
+    "ha": ("sbuf", [D, PER_CHIP * TK * (1 + MAX_A)], "bfloat16"),
+    "hb": ("sbuf", [D, PER_CHIP * TK * MAX_B], "bfloat16"),
+    "pa": ("sbuf", [D, TK * MAX_A], "bfloat16"),
+    "pb": ("sbuf", [D, TK * MAX_B], "bfloat16"),
+    "pin": ("sbuf", [D, TK * MAX_IN], "bfloat16"),
+    "t32": ("sbuf", [D, TK * MAX_IN], "float32"),
+    "ysb": ("sbuf", [D, TK], "bfloat16"),
+    "xd": ("dram", [D, TK], "bfloat16"),
+    "xr": ("dram", [D, TK], "bfloat16"),
+    "pha": ("psum", [D, 512], "float32"),
+    "pya": ("psum", [D, 512], "float32"),
+    "phb": ("psum", [D, 512], "float32"),
+    "pyb": ("psum", [D, 512], "float32"),
+}
+SEMAPHORES = ["xl", "xdl", "wl", "w", "xa", "xr", "xc", "xb", "pin0", "pin1", "pin2", "loc", "z",
+              "ha", "ra", "ya", "pa", "hb", "rb", "yb", "pb", "f", "yr", "st"]
+
+
+def _engines(mask):
+    return [e for e in range(mask.bit_length()) if (mask >> e) & 1]
+
+
+def _mask(engs):
+    m = 0
+    for e in engs:
+        m |= 1 << e
+    return m
+
+
+def _split(engs, k):
+    base = 1
+    while base * 2 * k <= len(engs):
+        base *= 2
+    sizes = [base] * k
+    for i in range(k):
+        if sum(sizes) + sizes[i] <= len(engs):
+            sizes[i] *= 2
+    out, at = [], 0
+    for s in sizes:
+        out.append(engs[at:at + s])
+        at += s
+    return out
+
+
+def _plan(cores, topo):
+    home = topo.chip
+    chips = []
+    for c in cores:
+        if home(c) not in chips:
+            chips.append(home(c))
+    on = {ch: [c for c in cores if home(c) == ch] for ch in chips}
+    idx = {c: i for i, c in enumerate(cores)}
+    serves = {c: any(topo.may_write(c, r) for r in cores if home(r) != home(c)) for c in cores}
+    load = {c: 0 for c in cores}
+    late = {c: 0 for c in cores}
+    duty = {c: 0 for c in cores}
+    jobs = []
+
+    def servers(r, ch):
+        return [p for p in on[ch] if p != r and serves[p] and topo.may_write(p, r)]
+
+    far = [(r, ch) for r in cores for ch in chips if ch != home(r)]
+    indirect = [(r, ch) for (r, ch) in far if not any(topo.may_write(r, p) for p in servers(r, ch))]
+    for (r, ch) in indirect:
+        p = min(servers(r, ch), key=lambda c: (late[c], load[c], idx[c]))
+        late[p] += 1
+        load[p] += 1
+        jobs.append({"own": r, "proc": p, "kind": "late", "relay": None})
+    for j in jobs:
+        q = min([c for c in on[home(j["own"])] if c != j["own"] and serves[c] and topo.may_write(c, j["proc"])],
+                key=lambda c: (duty[c], late[c], load[c], idx[c]))
+        duty[q] += 1
+        j["relay"] = q
+    for r in cores:
+        if not serves[r]:
+            q = [j["relay"] for j in jobs if j["own"] == r][0]
+            load[q] += 1
+            jobs.append({"own": r, "proc": q, "kind": "copy", "relay": None})
+    for (r, ch) in sorted([f for f in far if f not in indirect], key=lambda f: len(servers(f[0], f[1]))):
+        p = min([c for c in servers(r, ch) if topo.may_write(r, c)], key=lambda c: (load[c], idx[c]))
+        load[p] += 1
+        jobs.append({"own": r, "proc": p, "kind": "straight", "relay": None})
+
+    for c in cores:
+        grp_a = [j for j in jobs if j["proc"] == c and j["kind"] != "late"]
+        grp_b = [j for j in jobs if j["proc"] == c and j["kind"] == "late"]
+        assert len(grp_a) <= MAX_A and len(grp_b) <= MAX_B and duty[c] <= 1
+        away = _engines(topo.mask(c, [r for r in cores if home(r) != home(c)][0]))
+        near = [e for e in _engines(topo.mask(c, [r for r in on[home(c)] if r != c][0])) if e not in away]
+        for grp in (grp_a, grp_b):
+            for s, j in enumerate(grp):
+                j["xslot"] = s
+            out = [j for j in grp if home(j["own"]) != home(c)]
+            inn = [j for j in grp if home(j["own"]) == home(c)]
+            for part, engs in ((out, away), (inn, near)):
+                if part:
+                    for j, e in zip(part, _split(engs, len(part))):
+                        j["back"] = e
+        mine = sorted([j for j in jobs if j["own"] == c], key=lambda j: j["kind"] == "late")
+        assert len(mine) <= MAX_IN
+        for s, j in enumerate(mine):
+            j["pslot"] = s
+    return {"on": on, "serves": serves, "jobs": jobs}
+
+
+def rank_program(g, core, T, topo):
+    if T.rank_of(core) is None:
+        return
+    cores = list(T.cores)
+    plan = _plan(cores, topo)
+    jobs, S = plan["jobs"], T.sem
+    chipmates = plan["on"][topo.chip(core)]
+    peers = [c for c in chipmates if c != core]
+    serving = plan["serves"][core]
+    te, ve = g.tensor, g.vector
+    sent = [0]
+
+    def dst(c):
+        rid, pid, _ = topo.addr(c)
+        return DstId(rid=rid, pnc=pid)
+
+    def blk(t, s):
+        return t[:, s * TK:(s + 1) * TK]
+
+    def send(transfers):
+        g.remote_dma_fused(
+            [RemoteDMATransfer(dst_ids=[dst(c) for c, _ in to], dma_engine_mask=_mask(engs), remote_sem=sem,
+                               srcs=[src], dsts=[ap for _, ap in to]) for src, to, engs, sem in transfers],
+            local_sem=S.loc)
+        sent[0] += sum(len(engs) for _, _, engs, _ in transfers)
+
+    def handover_engines(r):
+        relays = [j["relay"] for j in jobs if j["own"] == r and j["kind"] == "late"]
+        away = _engines(topo.mask(r, [c for c in cores if topo.chip(c) != topo.chip(r)][0]))
+        engs = [e for e in _engines(topo.mask(r, relays[0])) if e not in away]
+        return engs[:2 * len(relays)]
+
+    grp_a = [j for j in jobs if j["proc"] == core and j["kind"] != "late"]
+    grp_b = [j for j in jobs if j["proc"] == core and j["kind"] == "late"]
+    mine = sorted([j for j in jobs if j["own"] == core], key=lambda j: j["pslot"])
+    handed = [j for j in mine if j["kind"] == "late"]
+    straight = [j for j in mine if j["kind"] == "straight"]
+    forward = [j for j in jobs if j["relay"] == core]
+    copied = [j for j in grp_a if j["kind"] == "copy"]
+    my = chipmates.index(core)
+    wslot = T.W[:, my * 2 * D:(my + 1) * 2 * D]
+
+    if handed:
+        g.sync.dma_start(T.xd[:], T.x[:]).then_inc(S.xdl, 16)
+        if serving:
+            g.scalar.dma_start(blk(T.xa, 0), T.x[:]).then_inc(S.xl, 16)
+    else:
+        g.sync.dma_start(blk(T.xa, 0), T.x[:]).then_inc(S.xl, 16)
+    g.scalar.dma_start(T.W[:, my * 2 * D:my * 2 * D + D], T.w1[:]).then_inc(S.wl, 16)
+    g.sync.dma_start(T.W[:, my * 2 * D + D:(my + 1) * 2 * D], T.w2[:]).then_inc(S.wl, 16)
+
+    if handed:
+        g.wait_ge(S.xdl, 16)
+        send([(T.xd[:], [(j["relay"], T.xr[:]) for j in handed], handover_engines(core), S.xr)])
+    if straight:
+        g.wait_ge(S.xl, 16)
+        send([(blk(T.xa, 0), [(j["proc"], blk(T.xa, 1 + j["xslot"])) for j in straight],
+               _engines(topo.mask(core, straight[0]["proc"])), S.xa)])
+    g.wait_ge(S.wl, 32)
+    wto = [c for c in peers if plan["serves"][c]]
+    send([(wslot, [(c, wslot) for c in wto], _engines(topo.mask(core, wto[0])), S.w)])
+    if forward:
+        g.wait_ge(S.xr, len(handover_engines(forward[0]["own"])))
+        for j in forward:
+            send([(T.xr[:], [(j["proc"], blk(T.xb, j["xslot"]))], _engines(topo.mask(core, j["proc"])), S.xb)])
+    if copied:
+        g.sync.wait_ge(S.xr, len(handover_engines(copied[0]["own"])))
+        g.sync.dma_start(blk(T.xa, 1 + copied[0]["xslot"]), T.xr[:]).then_inc(S.xc, 16)
+
+    if serving:
+        n_exp = len(chipmates)
+        ve.memset(T.zeros[:], 0.0).then_inc(S.z, 1)
+        ve.wait_ge(S.z, 1)
+        te.wait_ge(S.xl, 16)
+        te.wait_ge(S.wl, 32)
+        te.wait_ge(S.w, sum(len(_engines(topo.mask(c, core))) for c in peers))
+        n_straight = sum(len(_engines(topo.mask(j["own"], core))) for j in grp_a if j["kind"] == "straight")
+        if n_straight:
+            te.wait_ge(S.xa, n_straight)
+        if copied:
+            te.wait_ge(S.xc, 16)
+        groups = [(T.xa, TK * (1 + len(grp_a)), T.pha, T.ha, T.pya, S.ha, S.ra, S.ya, T.pa, S.pa, grp_a, TK)]
+        if grp_b:
+            groups.append((T.xb, TK * len(grp_b), T.phb, T.hb, T.pyb, S.hb, S.rb, S.yb, T.pb, S.pb, grp_b, 0))
+        for x_in, n, ph, h, py, s_h, s_r, s_y, p_out, s_p, grp, skip in groups:
+            if grp is grp_b:
+                te.wait_ge(S.xb, sum(len(_engines(topo.mask(j["relay"], core))) for j in grp_b))
+            for k in range(n_exp):
+                te.matmul(ph[:, k * n:(k + 1) * n], T.W[:, k * 2 * D:k * 2 * D + D], x_in[:, 0:n],
+                          True, True).then_inc(s_h, 1)
+            ve.wait_ge(s_h, n_exp)
+            ve.tensor_tensor(h[:, 0:n_exp * n], ph[:, 0:n_exp * n], T.zeros[:, 0:n_exp * n],
+                             AluOpType.max).then_inc(s_r, 1)
+            te.wait_ge(s_r, 1)
+            for k in range(n_exp):
+                te.matmul(py[:, 0:n], T.W[:, k * 2 * D + D:(k + 1) * 2 * D], h[:, k * n:(k + 1) * n],
+                          k == 0, k == n_exp - 1).then_inc(s_y, 1)
+            ve.wait_ge(s_y, n_exp)
+            if grp:
+                ve.tensor_copy(p_out[:, 0:n - skip], py[:, skip:n]).then_inc(s_p, 1)
+                g.wait_ge(s_p, 1)
+                send([(blk(p_out, j["xslot"]), [(j["own"], blk(T.pin, j["pslot"]))], j["back"],
+                       S["pin%d" % j["pslot"]]) for j in grp])
+
+    terms = ([(T.pya[:, 0:TK], None)] if serving else []) + [(blk(T.pin, j["pslot"]), j) for j in mine]
+    acc = None
+    for i, (t, j) in enumerate(terms):
+        if j is not None:
+            ve.wait_ge(S["pin%d" % j["pslot"]], len(j["back"]))
+        if i == 0:
+            acc = t
+            continue
+        last = i == len(terms) - 1
+        out = T.ysb[:] if last else blk(T.t32, i)
+        ins = ve.tensor_tensor(out, acc, t, AluOpType.add)
+        if last:
+            ins.then_inc(S.yr, 1)
+        else:
+            ins.then_inc(S.f, 1)
+            ve.wait_ge(S.f, i)
+        acc = out
+    g.sync.wait_ge(S.yr, 1)
+    g.sync.dma_start(T.y[:], T.ysb[:]).then_inc(S.st, 16)
+    g.sync.wait_ge(S.st, 16)
+    g.wait_ge(S.loc, sent[0])

@@ -1,5 +1,5 @@
 from concourse.bass import DstId, RemoteDMATransfer
-from concourse.mybir import AluOpType
+from concourse.mybir import AluOpType, ActivationFunctionType
 
 TK = 32
 D = 128
@@ -7,14 +7,17 @@ PER_CHIP = 4
 MAX_A = 3
 MAX_B = 2
 MAX_IN = 3
+MAX_LOAD = 3
 
 SCRATCH = {
-    "xa": ("sbuf", [D, TK * (1 + MAX_A)], "bfloat16"),
+    "xa": ("sbuf", [D, TK * MAX_A], "bfloat16"),
     "xb": ("sbuf", [D, TK * MAX_B], "bfloat16"),
+    "xc": ("sbuf", [D, TK], "bfloat16"),
     "W": ("sbuf", [D, 2 * D * PER_CHIP], "bfloat16"),
-    "zeros": ("sbuf", [D, 512], "float32"),
-    "ha": ("sbuf", [D, PER_CHIP * TK * (1 + MAX_A)], "bfloat16"),
+    "zeros": ("sbuf", [D, (PER_CHIP // 2) * TK * MAX_A], "float32"),
+    "ha": ("sbuf", [D, PER_CHIP * TK * MAX_A], "bfloat16"),
     "hb": ("sbuf", [D, PER_CHIP * TK * MAX_B], "bfloat16"),
+    "hc": ("sbuf", [D, PER_CHIP * TK], "bfloat16"),
     "pa": ("sbuf", [D, TK * MAX_A], "bfloat16"),
     "pb": ("sbuf", [D, TK * MAX_B], "bfloat16"),
     "pin": ("sbuf", [D, TK * MAX_IN], "bfloat16"),
@@ -22,13 +25,16 @@ SCRATCH = {
     "ysb": ("sbuf", [D, TK], "bfloat16"),
     "xd": ("dram", [D, TK], "bfloat16"),
     "xr": ("dram", [D, TK], "bfloat16"),
-    "pha": ("psum", [D, 512], "float32"),
+    "ph0": ("psum", [D, 512], "float32"),
+    "ph1": ("psum", [D, 512], "float32"),
     "pya": ("psum", [D, 512], "float32"),
-    "phb": ("psum", [D, 512], "float32"),
+    "phb0": ("psum", [D, 512], "float32"),
+    "phb1": ("psum", [D, 512], "float32"),
     "pyb": ("psum", [D, 512], "float32"),
+    "pyc": ("psum", [D, 512], "float32"),
 }
-SEMAPHORES = ["xl", "xdl", "wl", "w", "xa", "xr", "xc", "xb", "pin0", "pin1", "pin2", "loc", "z",
-              "ha", "ra", "ya", "pa", "hb", "rb", "yb", "pb", "f", "yr", "st"]
+SEMAPHORES = (["xl", "xdl", "wl", "w", "xa", "xr", "xn", "xb", "pin0", "pin1", "pin2", "loc", "z", "f", "yr", "st"]
+              + [s + t for t in "abc" for s in ("h0", "h1", "r0", "r1", "y", "p")])
 
 
 def _engines(mask):
@@ -74,35 +80,45 @@ def _plan(cores, topo):
     def servers(r, ch):
         return [p for p in on[ch] if p != r and serves[p] and topo.may_write(p, r)]
 
+    def off(a, b):
+        return topo.die(a) != topo.die(b)
+
     far = [(r, ch) for r in cores for ch in chips if ch != home(r)]
     indirect = [(r, ch) for (r, ch) in far if not any(topo.may_write(r, p) for p in servers(r, ch))]
     for (r, ch) in indirect:
-        p = min(servers(r, ch), key=lambda c: (late[c], load[c], idx[c]))
+        p = min(servers(r, ch), key=lambda c: (late[c], off(c, r), load[c], idx[c]))
         late[p] += 1
         load[p] += 1
         jobs.append({"own": r, "proc": p, "kind": "late", "relay": None})
     for j in jobs:
         q = min([c for c in on[home(j["own"])] if c != j["own"] and serves[c] and topo.may_write(c, j["proc"])],
-                key=lambda c: (duty[c], late[c], load[c], idx[c]))
+                key=lambda c: (duty[c], off(c, j["own"]), late[c], load[c], idx[c]))
         duty[q] += 1
         j["relay"] = q
     for r in cores:
         if not serves[r]:
-            q = [j["relay"] for j in jobs if j["own"] == r][0]
+            q = min(servers(r, home(r)), key=lambda c: (late[c], load[c], duty[c], idx[c]))
             load[q] += 1
-            jobs.append({"own": r, "proc": q, "kind": "copy", "relay": None})
-    for (r, ch) in sorted([f for f in far if f not in indirect], key=lambda f: len(servers(f[0], f[1]))):
-        p = min([c for c in servers(r, ch) if topo.may_write(r, c)], key=lambda c: (load[c], idx[c]))
+            jobs.append({"own": r, "proc": q, "kind": "near", "relay": None})
+
+    def cands(f):
+        return [c for c in servers(f[0], f[1]) if topo.may_write(f[0], c)]
+
+    def same(f):
+        return [c for c in cands(f) if not off(c, f[0])]
+
+    for f in sorted([f for f in far if f not in indirect], key=lambda f: (len(same(f)), len(cands(f)))):
+        p = min(cands(f), key=lambda c: (load[c] >= MAX_LOAD, off(c, f[0]), load[c], idx[c]))
         load[p] += 1
-        jobs.append({"own": r, "proc": p, "kind": "straight", "relay": None})
+        jobs.append({"own": f[0], "proc": p, "kind": "straight", "relay": None})
 
     for c in cores:
-        grp_a = [j for j in jobs if j["proc"] == c and j["kind"] != "late"]
-        grp_b = [j for j in jobs if j["proc"] == c and j["kind"] == "late"]
-        assert len(grp_a) <= MAX_A and len(grp_b) <= MAX_B and duty[c] <= 1
+        grps = [[j for j in jobs if j["proc"] == c and j["kind"] != "late"],
+                [j for j in jobs if j["proc"] == c and j["kind"] == "late"]]
+        assert len(grps[0]) <= MAX_A and len(grps[1]) <= MAX_B and duty[c] <= 1
         away = _engines(topo.mask(c, [r for r in cores if home(r) != home(c)][0]))
         near = [e for e in _engines(topo.mask(c, [r for r in on[home(c)] if r != c][0])) if e not in away]
-        for grp in (grp_a, grp_b):
+        for grp in grps:
             for s, j in enumerate(grp):
                 j["xslot"] = s
             out = [j for j in grp if home(j["own"]) != home(c)]
@@ -127,7 +143,7 @@ def rank_program(g, core, T, topo):
     chipmates = plan["on"][topo.chip(core)]
     peers = [c for c in chipmates if c != core]
     serving = plan["serves"][core]
-    te, ve = g.tensor, g.vector
+    te, ve, sc = g.tensor, g.vector, g.scalar
     sent = [0]
 
     def dst(c):
@@ -144,85 +160,94 @@ def rank_program(g, core, T, topo):
             local_sem=S.loc)
         sent[0] += sum(len(engs) for _, _, engs, _ in transfers)
 
+    def far_engines(r):
+        return _engines(topo.mask(r, [c for c in cores if topo.chip(c) != topo.chip(r)][0]))
+
+    def all_engines(r):
+        return _engines(topo.mask(r, [c for c in cores if topo.chip(c) == topo.chip(r) and c != r][0]))
+
     def handover_engines(r):
         relays = [j["relay"] for j in jobs if j["own"] == r and j["kind"] == "late"]
-        away = _engines(topo.mask(r, [c for c in cores if topo.chip(c) != topo.chip(r)][0]))
-        engs = [e for e in _engines(topo.mask(r, relays[0])) if e not in away]
-        return engs[:2 * len(relays)]
+        return [e for e in all_engines(r) if e not in far_engines(r)][:2 * len(relays)]
 
     grp_a = [j for j in jobs if j["proc"] == core and j["kind"] != "late"]
     grp_b = [j for j in jobs if j["proc"] == core and j["kind"] == "late"]
     mine = sorted([j for j in jobs if j["own"] == core], key=lambda j: j["pslot"])
     handed = [j for j in mine if j["kind"] == "late"]
     straight = [j for j in mine if j["kind"] == "straight"]
+    nearby = [j for j in mine if j["kind"] == "near"]
     forward = [j for j in jobs if j["relay"] == core]
-    copied = [j for j in grp_a if j["kind"] == "copy"]
     my = chipmates.index(core)
     wslot = T.W[:, my * 2 * D:(my + 1) * 2 * D]
 
-    if handed:
-        g.sync.dma_start(T.xd[:], T.x[:]).then_inc(S.xdl, 16)
-        if serving:
-            g.scalar.dma_start(blk(T.xa, 0), T.x[:]).then_inc(S.xl, 16)
-    else:
-        g.sync.dma_start(blk(T.xa, 0), T.x[:]).then_inc(S.xl, 16)
-    g.scalar.dma_start(T.W[:, my * 2 * D:my * 2 * D + D], T.w1[:]).then_inc(S.wl, 16)
+    g.sync.dma_start(T.xd[:], T.x[:]).then_inc(S.xdl, 16)
+    sc.dma_start(T.W[:, my * 2 * D:my * 2 * D + D], T.w1[:]).then_inc(S.wl, 16)
     g.sync.dma_start(T.W[:, my * 2 * D + D:(my + 1) * 2 * D], T.w2[:]).then_inc(S.wl, 16)
+    if serving:
+        g.sync.dma_start(T.xc[:], T.x[:]).then_inc(S.xl, 16)
 
+    g.wait_ge(S.xdl, 16)
     if handed:
-        g.wait_ge(S.xdl, 16)
         send([(T.xd[:], [(j["relay"], T.xr[:]) for j in handed], handover_engines(core), S.xr)])
     if straight:
-        g.wait_ge(S.xl, 16)
-        send([(blk(T.xa, 0), [(j["proc"], blk(T.xa, 1 + j["xslot"])) for j in straight],
-               _engines(topo.mask(core, straight[0]["proc"])), S.xa)])
+        send([(T.xd[:], [(j["proc"], blk(T.xa, j["xslot"])) for j in straight], far_engines(core), S.xa)])
+    for j in nearby:
+        send([(T.xd[:], [(j["proc"], blk(T.xa, j["xslot"]))], far_engines(core), S.xn)])
     g.wait_ge(S.wl, 32)
     wto = [c for c in peers if plan["serves"][c]]
-    send([(wslot, [(c, wslot) for c in wto], _engines(topo.mask(core, wto[0])), S.w)])
+    send([(wslot, [(c, wslot) for c in wto], all_engines(core), S.w)])
     if forward:
         g.wait_ge(S.xr, len(handover_engines(forward[0]["own"])))
         for j in forward:
-            send([(T.xr[:], [(j["proc"], blk(T.xb, j["xslot"]))], _engines(topo.mask(core, j["proc"])), S.xb)])
-    if copied:
-        g.sync.wait_ge(S.xr, len(handover_engines(copied[0]["own"])))
-        g.sync.dma_start(blk(T.xa, 1 + copied[0]["xslot"]), T.xr[:]).then_inc(S.xc, 16)
+            send([(T.xr[:], [(j["proc"], blk(T.xb, j["xslot"]))], far_engines(core), S.xb)])
 
     if serving:
         n_exp = len(chipmates)
+        half = n_exp // 2
         ve.memset(T.zeros[:], 0.0).then_inc(S.z, 1)
         ve.wait_ge(S.z, 1)
-        te.wait_ge(S.xl, 16)
         te.wait_ge(S.wl, 32)
-        te.wait_ge(S.w, sum(len(_engines(topo.mask(c, core))) for c in peers))
-        n_straight = sum(len(_engines(topo.mask(j["own"], core))) for j in grp_a if j["kind"] == "straight")
-        if n_straight:
-            te.wait_ge(S.xa, n_straight)
-        if copied:
-            te.wait_ge(S.xc, 16)
-        groups = [(T.xa, TK * (1 + len(grp_a)), T.pha, T.ha, T.pya, S.ha, S.ra, S.ya, T.pa, S.pa, grp_a, TK)]
-        if grp_b:
-            groups.append((T.xb, TK * len(grp_b), T.phb, T.hb, T.pyb, S.hb, S.rb, S.yb, T.pb, S.pb, grp_b, 0))
-        for x_in, n, ph, h, py, s_h, s_r, s_y, p_out, s_p, grp, skip in groups:
-            if grp is grp_b:
-                te.wait_ge(S.xb, sum(len(_engines(topo.mask(j["relay"], core))) for j in grp_b))
-            for k in range(n_exp):
-                te.matmul(ph[:, k * n:(k + 1) * n], T.W[:, k * 2 * D:k * 2 * D + D], x_in[:, 0:n],
-                          True, True).then_inc(s_h, 1)
-            ve.wait_ge(s_h, n_exp)
-            ve.tensor_tensor(h[:, 0:n_exp * n], ph[:, 0:n_exp * n], T.zeros[:, 0:n_exp * n],
-                             AluOpType.max).then_inc(s_r, 1)
-            te.wait_ge(s_r, 1)
-            for k in range(n_exp):
-                te.matmul(py[:, 0:n], T.W[:, k * 2 * D + D:(k + 1) * 2 * D], h[:, k * n:(k + 1) * n],
-                          k == 0, k == n_exp - 1).then_inc(s_y, 1)
-            ve.wait_ge(s_y, n_exp)
+        te.wait_ge(S.w, sum(len(all_engines(c)) for c in peers))
+        batches = [("a", T.xa, TK * len(grp_a), (T.ph0, T.ph1), T.ha, T.pya, T.pa, grp_a),
+                   ("b", T.xb, TK * len(grp_b), (T.phb0, T.phb1), T.hb, T.pyb, T.pb, grp_b),
+                   ("c", T.xc, TK, (T.ph0, T.ph1), T.hc, T.pyc, None, [])]
+        for tag, x_in, n, ph, h, py, p_out, grp in batches:
+            if n == 0:
+                continue
+            if tag == "a":
+                for kind, sem in (("straight", S.xa), ("near", S.xn)):
+                    due = sum(len(far_engines(j["own"])) for j in grp if j["kind"] == kind)
+                    if due:
+                        te.wait_ge(sem, due)
+            elif tag == "b":
+                te.wait_ge(S.xb, sum(len(far_engines(j["relay"])) for j in grp))
+            else:
+                te.wait_ge(S.xl, 16)
+            for hf in range(2):
+                for i in range(half):
+                    k = hf * half + i
+                    te.matmul(ph[hf][:, i * n:(i + 1) * n], T.W[:, k * 2 * D:k * 2 * D + D], x_in[:, 0:n],
+                              True, True).then_inc(S["h%d%s" % (hf, tag)], 1)
+            ve.wait_ge(S["h0" + tag], half)
+            ve.tensor_tensor(h[:, 0:half * n], ph[0][:, 0:half * n], T.zeros[:, 0:half * n],
+                             AluOpType.max).then_inc(S["r0" + tag], 1)
+            sc.wait_ge(S["h1" + tag], half)
+            sc.activation(h[:, half * n:2 * half * n], ph[1][:, 0:half * n],
+                          ActivationFunctionType.Relu).then_inc(S["r1" + tag], 1)
+            for hf in range(2):
+                te.wait_ge(S["r%d%s" % (hf, tag)], 1)
+                for i in range(half):
+                    k = hf * half + i
+                    te.matmul(py[:, 0:n], T.W[:, k * 2 * D + D:(k + 1) * 2 * D], h[:, k * n:(k + 1) * n],
+                              k == 0, k == n_exp - 1).then_inc(S["y" + tag], 1)
+            ve.wait_ge(S["y" + tag], n_exp)
             if grp:
-                ve.tensor_copy(p_out[:, 0:n - skip], py[:, skip:n]).then_inc(s_p, 1)
-                g.wait_ge(s_p, 1)
+                ve.tensor_copy(p_out[:, 0:n], py[:, 0:n]).then_inc(S["p" + tag], 1)
+                g.wait_ge(S["p" + tag], 1)
                 send([(blk(p_out, j["xslot"]), [(j["own"], blk(T.pin, j["pslot"]))], j["back"],
                        S["pin%d" % j["pslot"]]) for j in grp])
 
-    terms = ([(T.pya[:, 0:TK], None)] if serving else []) + [(blk(T.pin, j["pslot"]), j) for j in mine]
+    terms = ([(T.pyc[:, 0:TK], None)] if serving else []) + [(blk(T.pin, j["pslot"]), j) for j in mine]
     acc = None
     for i, (t, j) in enumerate(terms):
         if j is not None:

from concourse.bass import DstId, RemoteDMATransfer
from concourse.mybir import AluOpType, ActivationFunctionType

TK = 32
D = 128
PER_CHIP = 4
MAX_A = 3
MAX_B = 2
MAX_IN = 3
MAX_LOAD = 3

SCRATCH = {
    "xa": ("sbuf", [D, TK * MAX_A], "bfloat16"),
    "xb": ("sbuf", [D, TK * MAX_B], "bfloat16"),
    "xc": ("sbuf", [D, TK], "bfloat16"),
    "W": ("sbuf", [D, 2 * D * PER_CHIP], "bfloat16"),
    "zeros": ("sbuf", [D, (PER_CHIP // 2) * TK * MAX_A], "float32"),
    "ha": ("sbuf", [D, PER_CHIP * TK * MAX_A], "bfloat16"),
    "hb": ("sbuf", [D, PER_CHIP * TK * MAX_B], "bfloat16"),
    "hc": ("sbuf", [D, PER_CHIP * TK], "bfloat16"),
    "pa": ("sbuf", [D, TK * MAX_A], "bfloat16"),
    "pb": ("sbuf", [D, TK * MAX_B], "bfloat16"),
    "pin": ("sbuf", [D, TK * MAX_IN], "bfloat16"),
    "t32": ("sbuf", [D, TK * MAX_IN], "float32"),
    "ysb": ("sbuf", [D, TK], "bfloat16"),
    "xd": ("dram", [D, TK], "bfloat16"),
    "xr": ("dram", [D, TK], "bfloat16"),
    "ph0": ("psum", [D, 512], "float32"),
    "ph1": ("psum", [D, 512], "float32"),
    "pya": ("psum", [D, 512], "float32"),
    "phb0": ("psum", [D, 512], "float32"),
    "phb1": ("psum", [D, 512], "float32"),
    "pyb": ("psum", [D, 512], "float32"),
    "pyc": ("psum", [D, 512], "float32"),
}
SEMAPHORES = (["xl", "xdl", "wl", "w", "xa", "xr", "xn", "xb", "pin0", "pin1", "pin2", "loc", "z", "f", "yr", "st"]
              + [s + t for t in "abc" for s in ("h0", "h1", "r0", "r1", "y", "p")])


def _engines(mask):
    return [e for e in range(mask.bit_length()) if (mask >> e) & 1]


def _mask(engs):
    m = 0
    for e in engs:
        m |= 1 << e
    return m


def _split(engs, k):
    base = 1
    while base * 2 * k <= len(engs):
        base *= 2
    sizes = [base] * k
    for i in range(k):
        if sum(sizes) + sizes[i] <= len(engs):
            sizes[i] *= 2
    out, at = [], 0
    for s in sizes:
        out.append(engs[at:at + s])
        at += s
    return out


def _plan(cores, topo):
    home = topo.chip
    chips = []
    for c in cores:
        if home(c) not in chips:
            chips.append(home(c))
    on = {ch: [c for c in cores if home(c) == ch] for ch in chips}
    idx = {c: i for i, c in enumerate(cores)}
    serves = {c: any(topo.may_write(c, r) for r in cores if home(r) != home(c)) for c in cores}
    load = {c: 0 for c in cores}
    late = {c: 0 for c in cores}
    duty = {c: 0 for c in cores}
    jobs = []

    def servers(r, ch):
        return [p for p in on[ch] if p != r and serves[p] and topo.may_write(p, r)]

    def off(a, b):
        return topo.die(a) != topo.die(b)

    far = [(r, ch) for r in cores for ch in chips if ch != home(r)]
    indirect = [(r, ch) for (r, ch) in far if not any(topo.may_write(r, p) for p in servers(r, ch))]
    for (r, ch) in indirect:
        p = min(servers(r, ch), key=lambda c: (late[c], off(c, r), load[c], idx[c]))
        late[p] += 1
        load[p] += 1
        jobs.append({"own": r, "proc": p, "kind": "late", "relay": None})
    for j in jobs:
        q = min([c for c in on[home(j["own"])] if c != j["own"] and serves[c] and topo.may_write(c, j["proc"])],
                key=lambda c: (duty[c], off(c, j["own"]), late[c], load[c], idx[c]))
        duty[q] += 1
        j["relay"] = q
    for r in cores:
        if not serves[r]:
            q = min(servers(r, home(r)), key=lambda c: (late[c], load[c], duty[c], idx[c]))
            load[q] += 1
            jobs.append({"own": r, "proc": q, "kind": "near", "relay": None})

    def cands(f):
        return [c for c in servers(f[0], f[1]) if topo.may_write(f[0], c)]

    def same(f):
        return [c for c in cands(f) if not off(c, f[0])]

    for f in sorted([f for f in far if f not in indirect], key=lambda f: (len(same(f)), len(cands(f)))):
        p = min(cands(f), key=lambda c: (load[c] >= MAX_LOAD, off(c, f[0]), load[c], idx[c]))
        load[p] += 1
        jobs.append({"own": f[0], "proc": p, "kind": "straight", "relay": None})

    for c in cores:
        grps = [[j for j in jobs if j["proc"] == c and j["kind"] != "late"],
                [j for j in jobs if j["proc"] == c and j["kind"] == "late"]]
        assert len(grps[0]) <= MAX_A and len(grps[1]) <= MAX_B and duty[c] <= 1
        away = _engines(topo.mask(c, [r for r in cores if home(r) != home(c)][0]))
        near = [e for e in _engines(topo.mask(c, [r for r in on[home(c)] if r != c][0])) if e not in away]
        for grp in grps:
            for s, j in enumerate(grp):
                j["xslot"] = s
            out = [j for j in grp if home(j["own"]) != home(c)]
            inn = [j for j in grp if home(j["own"]) == home(c)]
            for part, engs in ((out, away), (inn, near)):
                if part:
                    for j, e in zip(part, _split(engs, len(part))):
                        j["back"] = e
        mine = sorted([j for j in jobs if j["own"] == c], key=lambda j: j["kind"] == "late")
        assert len(mine) <= MAX_IN
        for s, j in enumerate(mine):
            j["pslot"] = s
    return {"on": on, "serves": serves, "jobs": jobs}


def rank_program(g, core, T, topo):
    if T.rank_of(core) is None:
        return
    cores = list(T.cores)
    plan = _plan(cores, topo)
    jobs, S = plan["jobs"], T.sem
    chipmates = plan["on"][topo.chip(core)]
    peers = [c for c in chipmates if c != core]
    serving = plan["serves"][core]
    te, ve, sc = g.tensor, g.vector, g.scalar
    sent = [0]

    def dst(c):
        rid, pid, _ = topo.addr(c)
        return DstId(rid=rid, pnc=pid)

    def blk(t, s):
        return t[:, s * TK:(s + 1) * TK]

    def send(transfers):
        g.remote_dma_fused(
            [RemoteDMATransfer(dst_ids=[dst(c) for c, _ in to], dma_engine_mask=_mask(engs), remote_sem=sem,
                               srcs=[src], dsts=[ap for _, ap in to]) for src, to, engs, sem in transfers],
            local_sem=S.loc)
        sent[0] += sum(len(engs) for _, _, engs, _ in transfers)

    def far_engines(r):
        return _engines(topo.mask(r, [c for c in cores if topo.chip(c) != topo.chip(r)][0]))

    def all_engines(r):
        return _engines(topo.mask(r, [c for c in cores if topo.chip(c) == topo.chip(r) and c != r][0]))

    def handover_engines(r):
        relays = [j["relay"] for j in jobs if j["own"] == r and j["kind"] == "late"]
        return [e for e in all_engines(r) if e not in far_engines(r)][:2 * len(relays)]

    grp_a = [j for j in jobs if j["proc"] == core and j["kind"] != "late"]
    grp_b = [j for j in jobs if j["proc"] == core and j["kind"] == "late"]
    mine = sorted([j for j in jobs if j["own"] == core], key=lambda j: j["pslot"])
    handed = [j for j in mine if j["kind"] == "late"]
    straight = [j for j in mine if j["kind"] == "straight"]
    nearby = [j for j in mine if j["kind"] == "near"]
    forward = [j for j in jobs if j["relay"] == core]
    my = chipmates.index(core)
    wslot = T.W[:, my * 2 * D:(my + 1) * 2 * D]

    g.sync.dma_start(T.xd[:], T.x[:]).then_inc(S.xdl, 16)
    sc.dma_start(T.W[:, my * 2 * D:my * 2 * D + D], T.w1[:]).then_inc(S.wl, 16)
    g.sync.dma_start(T.W[:, my * 2 * D + D:(my + 1) * 2 * D], T.w2[:]).then_inc(S.wl, 16)
    if serving:
        g.sync.dma_start(T.xc[:], T.x[:]).then_inc(S.xl, 16)

    g.wait_ge(S.xdl, 16)
    if handed:
        send([(T.xd[:], [(j["relay"], T.xr[:]) for j in handed], handover_engines(core), S.xr)])
    if straight:
        send([(T.xd[:], [(j["proc"], blk(T.xa, j["xslot"])) for j in straight], far_engines(core), S.xa)])
    for j in nearby:
        send([(T.xd[:], [(j["proc"], blk(T.xa, j["xslot"]))], far_engines(core), S.xn)])
    g.wait_ge(S.wl, 32)
    wto = [c for c in peers if plan["serves"][c]]
    send([(wslot, [(c, wslot) for c in wto], all_engines(core), S.w)])
    if forward:
        g.wait_ge(S.xr, len(handover_engines(forward[0]["own"])))
        for j in forward:
            send([(T.xr[:], [(j["proc"], blk(T.xb, j["xslot"]))], far_engines(core), S.xb)])

    if serving:
        n_exp = len(chipmates)
        half = n_exp // 2
        ve.memset(T.zeros[:], 0.0).then_inc(S.z, 1)
        ve.wait_ge(S.z, 1)
        te.wait_ge(S.wl, 32)
        te.wait_ge(S.w, sum(len(all_engines(c)) for c in peers))
        batches = [("a", T.xa, TK * len(grp_a), (T.ph0, T.ph1), T.ha, T.pya, T.pa, grp_a),
                   ("b", T.xb, TK * len(grp_b), (T.phb0, T.phb1), T.hb, T.pyb, T.pb, grp_b),
                   ("c", T.xc, TK, (T.ph0, T.ph1), T.hc, T.pyc, None, [])]
        for tag, x_in, n, ph, h, py, p_out, grp in batches:
            if n == 0:
                continue
            if tag == "a":
                for kind, sem in (("straight", S.xa), ("near", S.xn)):
                    due = sum(len(far_engines(j["own"])) for j in grp if j["kind"] == kind)
                    if due:
                        te.wait_ge(sem, due)
            elif tag == "b":
                te.wait_ge(S.xb, sum(len(far_engines(j["relay"])) for j in grp))
            else:
                te.wait_ge(S.xl, 16)
            for hf in range(2):
                for i in range(half):
                    k = hf * half + i
                    te.matmul(ph[hf][:, i * n:(i + 1) * n], T.W[:, k * 2 * D:k * 2 * D + D], x_in[:, 0:n],
                              True, True).then_inc(S["h%d%s" % (hf, tag)], 1)
            ve.wait_ge(S["h0" + tag], half)
            ve.tensor_tensor(h[:, 0:half * n], ph[0][:, 0:half * n], T.zeros[:, 0:half * n],
                             AluOpType.max).then_inc(S["r0" + tag], 1)
            sc.wait_ge(S["h1" + tag], half)
            sc.activation(h[:, half * n:2 * half * n], ph[1][:, 0:half * n],
                          ActivationFunctionType.Relu).then_inc(S["r1" + tag], 1)
            for hf in range(2):
                te.wait_ge(S["r%d%s" % (hf, tag)], 1)
                for i in range(half):
                    k = hf * half + i
                    te.matmul(py[:, 0:n], T.W[:, k * 2 * D + D:(k + 1) * 2 * D], h[:, k * n:(k + 1) * n],
                              k == 0, k == n_exp - 1).then_inc(S["y" + tag], 1)
            ve.wait_ge(S["y" + tag], n_exp)
            if grp:
                ve.tensor_copy(p_out[:, 0:n], py[:, 0:n]).then_inc(S["p" + tag], 1)
                g.wait_ge(S["p" + tag], 1)
                send([(blk(p_out, j["xslot"]), [(j["own"], blk(T.pin, j["pslot"]))], j["back"],
                       S["pin%d" % j["pslot"]]) for j in grp])

    terms = ([(T.pyc[:, 0:TK], None)] if serving else []) + [(blk(T.pin, j["pslot"]), j) for j in mine]
    acc = None
    for i, (t, j) in enumerate(terms):
        if j is not None:
            ve.wait_ge(S["pin%d" % j["pslot"]], len(j["back"]))
        if i == 0:
            acc = t
            continue
        last = i == len(terms) - 1
        out = T.ysb[:] if last else blk(T.t32, i)
        ins = ve.tensor_tensor(out, acc, t, AluOpType.add)
        if last:
            ins.then_inc(S.yr, 1)
        else:
            ins.then_inc(S.f, 1)
            ve.wait_ge(S.f, i)
        acc = out
    g.sync.wait_ge(S.yr, 1)
    g.sync.dma_start(T.y[:], T.ysb[:]).then_inc(S.st, 16)
    g.sync.wait_ge(S.st, 16)
    g.wait_ge(S.loc, sent[0])
